import numpy as np
import ml_dtypes


def mxq(x, axis, fmt="e4m3"):
    dtype, down = {"e4m3": (ml_dtypes.float8_e4m3fn, 7), "e5m2": (ml_dtypes.float8_e5m2, 14)}[fmt]
    v = np.moveaxis(np.asarray(x, np.float32).astype(ml_dtypes.bfloat16).astype(np.float64), axis, -1)
    blocks = v.reshape(v.shape[:-1] + (-1, 32))
    amax = np.abs(blocks).max(-1, keepdims=True)
    byte = np.maximum(np.where(amax > 0, np.frexp(amax)[1] - 1 + 127, 0) - down, 1)
    scale = np.exp2(byte - 127.0)
    codes = (blocks / scale).astype(np.float32).astype(dtype).astype(np.float64)
    return np.moveaxis((codes * scale).reshape(v.shape), -1, axis)


WIDE = False


def mx_kscale(k):
    if not WIDE:
        return np.ones(k)
    levels = np.array([10, -10, 5, -5, 0])
    if k % 512:
        return np.exp2(np.random.permutation(np.resize(levels, k // 32))).repeat(32)
    a = np.empty((k // 512, 16))
    for p in range(k // 512):
        a[p, :8] = np.random.permutation(np.resize(levels, 8))
        for g in range(8):
            far = levels[np.abs(levels - a[p, g]) >= 10]
            a[p, g + 8] = far[np.random.randint(len(far))]
    return np.exp2(a.ravel()).repeat(32)


def f64(x):
    return np.asarray(x).astype(np.float64)


def striped(idx):
    return np.tile(idx.reshape(-1, 16).T, (8, 1)).astype(np.uint16)


def unstriped(offs):
    return offs[:16].T.reshape(-1).astype(np.int64)


def pack_weight(w):
    k, n = w.shape
    w = f64(np.asarray(w, np.float32).astype(ml_dtypes.bfloat16)).reshape(k // 32, 32, n)
    amax = np.abs(w).max(1)
    byte = np.clip(np.where(amax > 0, np.frexp(amax)[1] - 1 + 127 - 7, 1), 1, 254)
    scaled = (w * np.exp2(127.0 - byte)[:, None, :]).reshape(k, n).astype(np.float32)
    words = np.ascontiguousarray(scaled.reshape(k // 512, 128, 4, n).transpose(0, 1, 3, 2)).astype(ml_dtypes.float8_e4m3fn).view(np.uint8)
    return words, np.ascontiguousarray(byte.astype(np.uint8).reshape(k // 512, 16, n))


def unpack_weight(words, scales):
    g, p, n, _ = words.shape
    vals = np.ascontiguousarray(words).view(ml_dtypes.float8_e4m3fn).astype(np.float64) * np.repeat(np.exp2(scales.astype(np.float64) - 127.0), 8, axis=1)[..., None]
    return vals.transpose(0, 1, 3, 2).reshape(g * 512, n)


def planes(y):
    n, m = y.shape
    v = y.astype(np.float32).astype(ml_dtypes.bfloat16).astype(np.float64).reshape(n // 32, 32, m)
    top = np.abs(v).max(1)
    byte = np.clip(np.where(top > 0, np.frexp(top)[1] - 1 + 127 - 7, 1), 1, 254)
    codes = (v * np.exp2(127.0 - byte)[:, None, :]).reshape(n, m).astype(np.float32).astype(ml_dtypes.float8_e4m3fn).view(np.uint8)
    words = codes.reshape(n // 512, 128, 4, m).transpose(0, 1, 3, 2)
    return np.ascontiguousarray(words), np.ascontiguousarray(byte.astype(np.uint8).reshape(n // 512, 16, m))


K, T, S, D, H, N, V = 512, 2048, 1024, 2, 512, 512, 512


def setup_inputs():
    n = np.random.standard_normal
    s = mx_kscale(K)[:, None]
    u = mx_kscale(H)
    packed_xT = pack_weight(n((K, T)) * s)
    return {
        "x_words": packed_xT[0],
        "x_scales": packed_xT[1],
        "w1": (n((K, H)) / np.sqrt(K) / s * u).astype(np.float32),
        "t1": (n((H, N)) / np.sqrt(4 * H) / u[:, None]).astype(np.float32),
        "t2": (n((H, N)) / np.sqrt(4 * H) / u[:, None]).astype(np.float32),
        "t3": (n((H, N)) / np.sqrt(4 * H) / u[:, None]).astype(np.float32),
        "w2": (n((K, N)) / np.sqrt(4 * K) / s).astype(np.float32),
        "offs": striped(np.random.permutation(T)[:S]),
        "far1": striped(np.random.permutation(V)),
        "far2": striped(np.random.permutation(V)),
        "far3": striped(np.random.permutation(V)),
        "close": striped(np.random.permutation(T)[:V]),
    }


def reference(x_words, x_scales, w1, t1, t2, t3, w2, offs, far1, far2, far3, close):
    xq = unpack_weight(x_words, x_scales)[:, unstriped(offs)]
    y = mxq(f64(w1), 0, "e4m3").T @ xq
    h = y.reshape(len(y), -1, D).sum(axis=2)
    m0 = h[:, unstriped(far1)]
    m1 = h[:, unstriped(far2)]
    m2 = h[:, unstriped(far3)]
    x_close = unpack_weight(x_words, x_scales)[:, unstriped(close)]
    out_0 = mxq(f64(t1), 0, "e4m3").T @ mxq(m0, 0, "e4m3") + mxq(f64(t2), 0, "e4m3").T @ mxq(m1, 0, "e4m3") + mxq(f64(t3), 0, "e4m3").T @ mxq(m2, 0, "e4m3") + mxq(f64(w2), 0, "e4m3").T @ x_close
    return (out_0,) + planes(out_0)

@@ -1,0 +1,243 @@
+from contextlib import ExitStack
+
+import concourse.mybir as mybir
+
+K, T, S, D, H, N, V = 512, 2048, 1024, 2, 512, 512, 512
+FLOPS = 2 * K * H * S + 3 * 2 * H * N * V + 2 * K * N * V
+
+F32 = mybir.dt.float32
+BF16 = mybir.dt.bfloat16
+I32 = mybir.dt.int32
+U32 = mybir.dt.uint32
+U16 = mybir.dt.uint16
+U8 = mybir.dt.uint8
+FP8X4 = mybir.dt.float8_e4m3fn_x4
+
+P = 128
+PACK = 4
+HALF = 256
+SLOT = [0, 1, 2, 0, 1, 0, 1, 0, 1]
+CHUNKS = [(0, 256), (256, 128), (384, 128)]
+
+
+def tile_picked_yfmm_none_po_kernel(tc, x_words, x_scales, w1, t1, t2, t3, w2, offs, far1, far2, far3, close, out_0, out_1, out_2):
+    nc = tc.nc
+    with ExitStack() as ctx:
+        keep = ctx.enter_context(tc.tile_pool(name="keep", bufs=1))
+        ring = ctx.enter_context(tc.tile_pool(name="ring", bufs=1))
+        psum = ctx.enter_context(tc.psum_pool(name="psum", bufs=2))
+
+        def load_list(src, name):
+            tile = keep.tile(list(src.shape), U16, name=name)
+            nc.sync.dma_start(tile[:], src)
+            return tile
+
+        def load_weight(w, name):
+            raw = ring.tile([P, PACK, 2 * HALF], F32, name=f"{name}_raw", tag=f"{name}_raw", align_bytes=64)
+            nc.sync.dma_start(raw[:], w.rearrange("(p j) c -> p j c", j=PACK))
+            return [raw[:, :, u * HALF : (u + 1) * HALF] for u in range(2)]
+
+        def deal_half(copy, raw_half, dealt, u):
+            m_cols = slice(u * 64, (u + 1) * 64)
+            copy(
+                dealt[:].rearrange("p (t m j) -> p m j t", t=PACK, j=PACK)[:, m_cols],
+                raw_half.rearrange("p j (m t) -> p m j t", t=PACK),
+            )
+
+        def quantize(src, width, pool, name, bufs):
+            codes = pool.tile([P, width], U32, name=f"{name}_codes", align_bytes=64, bufs=bufs)
+            scales = pool.tile([P, width], U8, name=f"{name}_scales", align_bytes=64, bufs=bufs)
+            nc.vector.quantize_mx(out=codes[:].bitcast(FP8X4), scales=scales[:], in_=src)
+            return codes, scales
+
+        def product(acc, weight, t, moving_codes, moving_scales, start, stop):
+            cols = slice(t * P, (t + 1) * P)
+            nc.tensor.matmul_mx(
+                out=acc,
+                lhsT=weight[0][:, cols].bitcast(FP8X4),
+                lhsT_scale=weight[1][:, cols],
+                rhs=moving_codes.bitcast(FP8X4),
+                rhs_scale=moving_scales,
+                start=start,
+                stop=stop,
+            )
+
+        table_scales = keep.tile([P, T], U8, name="table_scales")
+        nc.vector.memset(table_scales[:].bitcast(I32), 0)
+        offs_sb = load_list(offs, "offs_sb")
+        for q in range(4):
+            nc.sync.dma_start(
+                table_scales[32 * q : 32 * q + 4, :].bitcast(I32), x_scales[0][4 * q : 4 * q + 4, :].bitcast(I32)
+            )
+        w1_raw = load_weight(w1, "w1")
+        table_words = keep.tile([P, T], U32, name="table_words")
+        nc.sync.dma_start(table_words[:].bitcast(I32), x_words[0].rearrange("p n t -> p (n t)").bitcast(I32))
+        w2_raw = load_weight(w2, "w2")
+        close_sb = load_list(close, "close_sb")
+        far_sb = [load_list(far1, "far1_sb"), load_list(far2, "far2_sb"), load_list(far3, "far3_sb")]
+        t_raw = [load_weight(t1, "t1")]
+        t_raw.append(load_weight(t2, "t2"))
+        t_raw.append(load_weight(t3, "t3"))
+
+        dealt = {name: keep.tile([P, PACK * H], BF16, name=f"{name}_dealt", align_bytes=64) for name in ("w1", "w2", "t1", "t2", "t3")}
+
+        for u in range(2):
+            deal_half(nc.scalar.copy, w1_raw[u], dealt["w1"], u)
+        picked_scales = keep.tile([P, S], U8, name="picked_scales")
+        nc.vector.tensor_copy(picked_scales[:], table_scales[:].indirect(offs_sb[:]))
+        pair_scales = keep.tile([P, D, V], U8, name="pair_scales", align_bytes=64)
+        nc.vector.tensor_copy(pair_scales[:].rearrange("p d v -> p v d"), picked_scales[:].rearrange("p (v d) -> p v d", d=D))
+
+        h_banks = [psum.tile([P, V], F32, name=f"h_bank{t}", tag=f"bank{t}") for t in range(PACK)]
+        pair_words = [
+            ring.tile([P, D, HALF], U32, name=f"pair_words{u}", tag=tag, align_bytes=64)
+            for u, tag in enumerate(("pair_words", "w1_raw"))
+        ]
+
+        def gather_pairs(u):
+            nc.vector.tensor_copy(
+                pair_words[u][:].rearrange("p d v -> p v d"), table_words[:].indirect(offs_sb[:, u * 32 : (u + 1) * 32])
+            )
+
+        gather_pairs(0)
+        w1_q = quantize(dealt["w1"][:], H, keep, "w1", 1)
+        gather_pairs(1)
+        for t, u in ((0, 0), (1, 0), (0, 1), (1, 1), (2, 0), (2, 1), (3, 0), (3, 1)):
+            cols = slice(u * HALF, (u + 1) * HALF)
+            for d in range(D):
+                product(h_banks[t][:, cols], w1_q, t, pair_words[u][:, d, :], pair_scales[:, d, cols], d == 0, d == D - 1)
+        for u in range(2):
+            deal_half(nc.scalar.copy, w2_raw[u], dealt["w2"], u)
+        close_scales = keep.tile([P, V], U8, name="close_scales", align_bytes=64)
+        nc.vector.tensor_copy(close_scales[:], table_scales[:].indirect(close_sb[:]))
+        close_words = keep.tile([P, V], U32, name="close_words", align_bytes=64)
+        nc.vector.tensor_copy(close_words[:], table_words[:].indirect(close_sb[:]))
+        h = []
+        for t in range(PACK):
+            h.append(keep.tile([P, V], F32, name=f"h{t}"))
+            nc.scalar.copy(h[t][:], h_banks[t][:])
+
+        steps = [(c, l) for c in range(len(CHUNKS)) for l in range(3)]
+        gathered, rounded, banks, t_q, results, stored = {}, {}, {}, {}, {}, {}
+
+        def gather(s, t):
+            c, l = steps[s]
+            v0, n = CHUNKS[c]
+            if s not in gathered:
+                gathered[s] = ring.tile([P, PACK, n], F32, name=f"gathered{s}", tag=f"gathered{SLOT[s]}", align_bytes=64)
+            nc.vector.tensor_copy(gathered[s][:, t, :], h[t][:].indirect(far_sb[l][:, v0 // 16 : (v0 + n) // 16]))
+
+        def weave(copy, src, dst):
+            copy(
+                dst.rearrange("p (c i t) -> p c t i", i=4, t=PACK),
+                src[:].rearrange("p t (c i) -> p c t i", i=4),
+            )
+
+        def round_moments(s, copy):
+            n = CHUNKS[steps[s][0]][1]
+            if s < 3:
+                if s == 0:
+                    rounded["first"] = ring.tile([P, 3, PACK * n], BF16, name="rounded_first", tag="t3_raw", align_bytes=64)
+                rounded[s] = rounded["first"][:, s, :]
+            elif s == 8:
+                rounded[s] = ring.tile([P, PACK * n], BF16, name="rounded_last", tag=f"gathered{SLOT[7]}", align_bytes=64)[:]
+            else:
+                rounded[s] = ring.tile([P, PACK * n], BF16, name="rounded", align_bytes=64, bufs=3)[:]
+            weave(copy, gathered[s], rounded[s])
+
+        def open_chunk(c):
+            v0, n = CHUNKS[c]
+            banks[c] = [psum.tile([P, n], F32, name=f"out_bank{t}", tag=f"bank{t}") for t in range(PACK)]
+            for t in range(PACK):
+                product(banks[c][t][:], w2_q, t, close_words[:, v0 : v0 + n], close_scales[:, v0 : v0 + n], True, False)
+
+        def multiply(s):
+            c, l = steps[s]
+            n = CHUNKS[c][1]
+            codes, scales = quantize(rounded[s], n, ring, "m", 3)
+            for t in range(PACK):
+                product(banks[c][t][:], t_q[l], t, codes[:], scales[:], False, l == 2)
+
+        def deal_t(l, u):
+            deal_half(nc.scalar.copy, t_raw[l][u], dealt[f"t{l + 1}"], u)
+
+        def quantize_t(l):
+            t_q[l] = quantize(dealt[f"t{l + 1}"][:], N, keep, f"t{l + 1}", 1)
+
+        out_scales = keep.tile([P, V], U8, name="out_scales", align_bytes=64)
+
+        def drain(c, copies):
+            v0, n = CHUNKS[c]
+            result = keep.tile([P, PACK, n], F32, name=f"result{c}")
+            for t in range(PACK):
+                copies[t](result[:, t, :], banks[c][t][:])
+            nc.sync.dma_start(out_0.rearrange("(p t) v -> p t v", t=PACK)[:, :, v0 : v0 + n], result[:])
+            results[c] = keep.tile([P, PACK * n], BF16, name=f"result_bf{c}", align_bytes=64)
+            stored[c] = result
+
+        def round_result(c, copy):
+            weave(copy, stored[c], results[c][:])
+
+        def hand_on(c):
+            v0, n = CHUNKS[c]
+            words = keep.tile([P, n], U32, name=f"out_words{c}", align_bytes=64)
+            nc.vector.quantize_mx(out=words[:].bitcast(FP8X4), scales=out_scales[:, v0 : v0 + n], in_=results[c][:])
+            nc.sync.dma_start(
+                out_1[0].rearrange("p n t -> p (n t)").bitcast(I32)[:, v0 : v0 + n], words[:].bitcast(I32)
+            )
+
+        sc, ve = nc.scalar.copy, nc.vector.tensor_copy
+
+        def gather_all(s):
+            for t in range(PACK):
+                gather(s, t)
+
+        for t in range(PACK):
+            for s in range(3):
+                gather(s, t)
+        w2_q = quantize(dealt["w2"][:], N, keep, "w2", 1)
+        open_chunk(0)
+        for l in range(3):
+            deal_t(l, 0)
+            deal_t(l, 1)
+        for s in range(3):
+            round_moments(s, sc)
+        for l in range(3):
+            quantize_t(l)
+        multiply(0)
+        gather_all(3)
+        multiply(1)
+        gather_all(4)
+        round_moments(3, sc)
+        multiply(2)
+        open_chunk(1)
+        round_moments(4, sc)
+        multiply(3)
+        gather_all(5)
+        drain(0, [sc] * 4)
+        round_moments(5, sc)
+        multiply(4)
+        gather_all(6)
+        round_moments(6, sc)
+        round_result(0, sc)
+        multiply(5)
+        open_chunk(2)
+        gather_all(7)
+        round_moments(7, sc)
+        drain(1, [sc] * 4)
+        round_result(1, sc)
+        multiply(6)
+        gather_all(8)
+        multiply(7)
+        round_moments(8, ve)
+        multiply(8)
+        hand_on(0)
+        hand_on(1)
+        drain(2, [sc, ve, sc, ve])
+        round_result(2, ve)
+        hand_on(2)
+        for q in range(4):
+            queue = nc.scalar if q % 2 else nc.sync
+            queue.dma_start(
+                out_2[0][4 * q : 4 * q + 4, :].bitcast(I32), out_scales[32 * q : 32 * q + 4, :].bitcast(I32)
+            )

@@ -16,7 +16,8 @@ FP8X4 = mybir.dt.float8_e4m3fn_x4
 P = 128
 PACK = 4
 HALF = 256
-SLOT = [0, 1, 2, 0, 1, 0, 1, 0, 1]
+STEPS = [(0, 0, 256), (1, 0, 256), (2, 0, 256), (0, 256, 256), (1, 256, 256), (2, 256, 128), (2, 384, 128)]
+SLOT = [0, 1, 2, 0, 2, 0, 2]
 CHUNKS = [(0, 256), (256, 128), (384, 128)]
 
 
@@ -31,6 +32,11 @@ def tile_picked_yfmm_none_po_kernel(tc, x_words, x_scales, w1, t1, t2, t3, w2, o
             tile = keep.tile(list(src.shape), U16, name=name)
             nc.sync.dma_start(tile[:], src)
             return tile
+
+        def load_weight_half(w, u, name):
+            raw = ring.tile([P, PACK, HALF], F32, name=f"{name}_raw{u}", align_bytes=64)
+            nc.sync.dma_start(raw[:], w.rearrange("(p j) c -> p j c", j=PACK)[:, :, u * HALF : (u + 1) * HALF])
+            return raw[:]
 
         def load_weight(w, name):
             raw = ring.tile([P, PACK, 2 * HALF], F32, name=f"{name}_raw", tag=f"{name}_raw", align_bytes=64)
@@ -65,16 +71,18 @@ def tile_picked_yfmm_none_po_kernel(tc, x_words, x_scales, w1, t1, t2, t3, w2, o
         table_scales = keep.tile([P, T], U8, name="table_scales")
         nc.vector.memset(table_scales[:].bitcast(I32), 0)
         offs_sb = load_list(offs, "offs_sb")
+        close_sb = load_list(close, "close_sb")
+        far_sb = [load_list(far1, "far1_sb")]
         for q in range(4):
-            nc.sync.dma_start(
+            (nc.scalar if q % 2 else nc.sync).dma_start(
                 table_scales[32 * q : 32 * q + 4, :].bitcast(I32), x_scales[0][4 * q : 4 * q + 4, :].bitcast(I32)
             )
         w1_raw = load_weight(w1, "w1")
+        w2_raw = [load_weight_half(w2, 0, "w2")]
         table_words = keep.tile([P, T], U32, name="table_words")
         nc.sync.dma_start(table_words[:].bitcast(I32), x_words[0].rearrange("p n t -> p (n t)").bitcast(I32))
-        w2_raw = load_weight(w2, "w2")
-        close_sb = load_list(close, "close_sb")
-        far_sb = [load_list(far1, "far1_sb"), load_list(far2, "far2_sb"), load_list(far3, "far3_sb")]
+        w2_raw.append(load_weight_half(w2, 1, "w2"))
+        far_sb.extend([load_list(far2, "far2_sb"), load_list(far3, "far3_sb")])
         t_raw = [load_weight(t1, "t1")]
         t_raw.append(load_weight(t2, "t2"))
         t_raw.append(load_weight(t3, "t3"))
@@ -83,46 +91,38 @@ def tile_picked_yfmm_none_po_kernel(tc, x_words, x_scales, w1, t1, t2, t3, w2, o
 
         for u in range(2):
             deal_half(nc.scalar.copy, w1_raw[u], dealt["w1"], u)
+        deal_half(nc.scalar.copy, w2_raw[0], dealt["w2"], 0)
         picked_scales = keep.tile([P, S], U8, name="picked_scales")
         nc.vector.tensor_copy(picked_scales[:], table_scales[:].indirect(offs_sb[:]))
+        close_scales = keep.tile([P, V], U8, name="close_scales", align_bytes=64)
+        nc.vector.tensor_copy(close_scales[:], table_scales[:].indirect(close_sb[:]))
         pair_scales = keep.tile([P, D, V], U8, name="pair_scales", align_bytes=64)
         nc.vector.tensor_copy(pair_scales[:].rearrange("p d v -> p v d"), picked_scales[:].rearrange("p (v d) -> p v d", d=D))
+        w1_q = quantize(dealt["w1"][:], H, keep, "w1", 1)
 
         h_banks = [psum.tile([P, V], F32, name=f"h_bank{t}", tag=f"bank{t}") for t in range(PACK)]
-        pair_words = [
-            ring.tile([P, D, HALF], U32, name=f"pair_words{u}", tag=tag, align_bytes=64)
-            for u, tag in enumerate(("pair_words", "w1_raw"))
-        ]
-
-        def gather_pairs(u):
+        pair_words = [keep.tile([P, D, HALF], U32, name=f"pair_words{u}", align_bytes=64) for u in range(2)]
+        for u in range(2):
             nc.vector.tensor_copy(
                 pair_words[u][:].rearrange("p d v -> p v d"), table_words[:].indirect(offs_sb[:, u * 32 : (u + 1) * 32])
             )
-
-        gather_pairs(0)
-        w1_q = quantize(dealt["w1"][:], H, keep, "w1", 1)
-        gather_pairs(1)
         for t, u in ((0, 0), (1, 0), (0, 1), (1, 1), (2, 0), (2, 1), (3, 0), (3, 1)):
             cols = slice(u * HALF, (u + 1) * HALF)
             for d in range(D):
                 product(h_banks[t][:, cols], w1_q, t, pair_words[u][:, d, :], pair_scales[:, d, cols], d == 0, d == D - 1)
-        for u in range(2):
-            deal_half(nc.scalar.copy, w2_raw[u], dealt["w2"], u)
-        close_scales = keep.tile([P, V], U8, name="close_scales", align_bytes=64)
-        nc.vector.tensor_copy(close_scales[:], table_scales[:].indirect(close_sb[:]))
+        deal_half(nc.scalar.copy, w2_raw[1], dealt["w2"], 1)
         close_words = keep.tile([P, V], U32, name="close_words", align_bytes=64)
         nc.vector.tensor_copy(close_words[:], table_words[:].indirect(close_sb[:]))
         h = []
         for t in range(PACK):
             h.append(keep.tile([P, V], F32, name=f"h{t}"))
             nc.scalar.copy(h[t][:], h_banks[t][:])
+        w2_q = quantize(dealt["w2"][:], N, keep, "w2", 1)
 
-        steps = [(c, l) for c in range(len(CHUNKS)) for l in range(3)]
-        gathered, rounded, banks, t_q, results, stored = {}, {}, {}, {}, {}, {}
+        gathered, rounded, moments, banks, t_q, results, stored = {}, {}, {}, {}, {}, {}, {}
 
         def gather(s, t):
-            c, l = steps[s]
-            v0, n = CHUNKS[c]
+            l, v0, n = STEPS[s]
             if s not in gathered:
                 gathered[s] = ring.tile([P, PACK, n], F32, name=f"gathered{s}", tag=f"gathered{SLOT[s]}", align_bytes=64)
             nc.vector.tensor_copy(gathered[s][:, t, :], h[t][:].indirect(far_sb[l][:, v0 // 16 : (v0 + n) // 16]))
@@ -133,17 +133,12 @@ def tile_picked_yfmm_none_po_kernel(tc, x_words, x_scales, w1, t1, t2, t3, w2, o
                 src[:].rearrange("p t (c i) -> p c t i", i=4),
             )
 
-        def round_moments(s, copy):
-            n = CHUNKS[steps[s][0]][1]
-            if s < 3:
-                if s == 0:
-                    rounded["first"] = ring.tile([P, 3, PACK * n], BF16, name="rounded_first", tag="t3_raw", align_bytes=64)
-                rounded[s] = rounded["first"][:, s, :]
-            elif s == 8:
-                rounded[s] = ring.tile([P, PACK * n], BF16, name="rounded_last", tag=f"gathered{SLOT[7]}", align_bytes=64)[:]
-            else:
-                rounded[s] = ring.tile([P, PACK * n], BF16, name="rounded", align_bytes=64, bufs=3)[:]
-            weave(copy, gathered[s], rounded[s])
+        def round_moments(first, count, tag, copy):
+            n = STEPS[first][2]
+            tile = ring.tile([P, count, PACK * n], BF16, name=f"rounded{first}", tag=tag, align_bytes=64)
+            for i in range(count):
+                rounded[first + i] = tile[:, i, :]
+                weave(copy, gathered[first + i], rounded[first + i])
 
         def open_chunk(c):
             v0, n = CHUNKS[c]
@@ -151,12 +146,16 @@ def tile_picked_yfmm_none_po_kernel(tc, x_words, x_scales, w1, t1, t2, t3, w2, o
             for t in range(PACK):
                 product(banks[c][t][:], w2_q, t, close_words[:, v0 : v0 + n], close_scales[:, v0 : v0 + n], True, False)
 
-        def multiply(s):
-            c, l = steps[s]
-            n = CHUNKS[c][1]
-            codes, scales = quantize(rounded[s], n, ring, "m", 3)
+        def quantize_moments(s):
+            moments[s] = quantize(rounded[s], STEPS[s][2], keep, f"m{s}", 1)
+
+        def multiply(s, c):
+            l, s0, width = STEPS[s]
+            v0, n = CHUNKS[c]
+            cols = slice(v0 - s0, v0 - s0 + n)
+            codes, scales = moments[s]
             for t in range(PACK):
-                product(banks[c][t][:], t_q[l], t, codes[:], scales[:], False, l == 2)
+                product(banks[c][t][:], t_q[l], t, codes[:, cols], scales[:, cols], False, l == 2)
 
         def deal_t(l, u):
             deal_half(nc.scalar.copy, t_raw[l][u], dealt[f"t{l + 1}"], u)
@@ -195,45 +194,49 @@ def tile_picked_yfmm_none_po_kernel(tc, x_words, x_scales, w1, t1, t2, t3, w2, o
         for t in range(PACK):
             for s in range(3):
                 gather(s, t)
-        w2_q = quantize(dealt["w2"][:], N, keep, "w2", 1)
         open_chunk(0)
-        for l in range(3):
+        for l in range(2):
             deal_t(l, 0)
             deal_t(l, 1)
-        for s in range(3):
-            round_moments(s, sc)
-        for l in range(3):
-            quantize_t(l)
-        multiply(0)
+        round_moments(0, 2, "t2_raw", sc)
+        deal_t(2, 0)
+        deal_t(2, 1)
+        quantize_t(0)
+        quantize_t(1)
+        quantize_moments(0)
+        multiply(0, 0)
         gather_all(3)
-        multiply(1)
+        round_moments(2, 2, "t3_raw", sc)
+        quantize_moments(1)
+        multiply(1, 0)
+        quantize_t(2)
+        quantize_moments(2)
+        multiply(2, 0)
         gather_all(4)
-        round_moments(3, sc)
-        multiply(2)
         open_chunk(1)
-        round_moments(4, sc)
-        multiply(3)
-        gather_all(5)
         drain(0, [sc] * 4)
-        round_moments(5, sc)
-        multiply(4)
-        gather_all(6)
-        round_moments(6, sc)
-        round_result(0, sc)
-        multiply(5)
         open_chunk(2)
-        gather_all(7)
-        round_moments(7, sc)
+        quantize_moments(3)
+        round_moments(4, 1, "t3_raw", sc)
+        multiply(3, 1)
+        multiply(3, 2)
+        gather_all(5)
+        round_moments(5, 1, "rounded5", sc)
+        round_result(0, sc)
+        quantize_moments(4)
+        multiply(4, 1)
+        multiply(4, 2)
+        gather_all(6)
+        quantize_moments(5)
+        multiply(5, 1)
+        round_moments(6, 1, f"gathered{SLOT[5]}", ve)
         drain(1, [sc] * 4)
-        round_result(1, sc)
-        multiply(6)
-        gather_all(8)
-        multiply(7)
-        round_moments(8, ve)
-        multiply(8)
+        quantize_moments(6)
+        multiply(6, 2)
         hand_on(0)
-        hand_on(1)
+        round_result(1, ve)
         drain(2, [sc, ve, sc, ve])
+        hand_on(1)
         round_result(2, ve)
         hand_on(2)
         for q in range(4):

@@ -33,11 +33,6 @@ def tile_picked_yfmm_none_po_kernel(tc, x_words, x_scales, w1, t1, t2, t3, w2, o
             nc.sync.dma_start(tile[:], src)
             return tile
 
-        def load_weight_half(w, u, name):
-            raw = ring.tile([P, PACK, HALF], F32, name=f"{name}_raw{u}", align_bytes=64)
-            nc.sync.dma_start(raw[:], w.rearrange("(p j) c -> p j c", j=PACK)[:, :, u * HALF : (u + 1) * HALF])
-            return raw[:]
-
         def load_weight(w, name):
             raw = ring.tile([P, PACK, 2 * HALF], F32, name=f"{name}_raw", tag=f"{name}_raw", align_bytes=64)
             nc.sync.dma_start(raw[:], w.rearrange("(p j) c -> p j c", j=PACK))
@@ -78,46 +73,51 @@ def tile_picked_yfmm_none_po_kernel(tc, x_words, x_scales, w1, t1, t2, t3, w2, o
                 table_scales[32 * q : 32 * q + 4, :].bitcast(I32), x_scales[0][4 * q : 4 * q + 4, :].bitcast(I32)
             )
         w1_raw = load_weight(w1, "w1")
-        w2_raw = [load_weight_half(w2, 0, "w2")]
         table_words = keep.tile([P, T], U32, name="table_words")
         nc.sync.dma_start(table_words[:].bitcast(I32), x_words[0].rearrange("p n t -> p (n t)").bitcast(I32))
-        w2_raw.append(load_weight_half(w2, 1, "w2"))
+        w2_raw = load_weight(w2, "w2")
         far_sb.extend([load_list(far2, "far2_sb"), load_list(far3, "far3_sb")])
         t_raw = [load_weight(t1, "t1")]
         t_raw.append(load_weight(t2, "t2"))
         t_raw.append(load_weight(t3, "t3"))
 
-        dealt = {name: keep.tile([P, PACK * H], BF16, name=f"{name}_dealt", align_bytes=64) for name in ("w1", "w2", "t1", "t2", "t3")}
+        dealt = {name: ring.tile([P, PACK * H], BF16, name=f"{name}_dealt", tag=f"{name}_dealt", align_bytes=64) for name in ("w1", "w2", "t1", "t2", "t3")}
 
         for u in range(2):
             deal_half(nc.scalar.copy, w1_raw[u], dealt["w1"], u)
-        deal_half(nc.scalar.copy, w2_raw[0], dealt["w2"], 0)
         picked_scales = keep.tile([P, S], U8, name="picked_scales")
         nc.vector.tensor_copy(picked_scales[:], table_scales[:].indirect(offs_sb[:]))
         close_scales = keep.tile([P, V], U8, name="close_scales", align_bytes=64)
         nc.vector.tensor_copy(close_scales[:], table_scales[:].indirect(close_sb[:]))
         pair_scales = keep.tile([P, D, V], U8, name="pair_scales", align_bytes=64)
         nc.vector.tensor_copy(pair_scales[:].rearrange("p d v -> p v d"), picked_scales[:].rearrange("p (v d) -> p v d", d=D))
-        w1_q = quantize(dealt["w1"][:], H, keep, "w1", 1)
 
         h_banks = [psum.tile([P, V], F32, name=f"h_bank{t}", tag=f"bank{t}") for t in range(PACK)]
-        pair_words = [keep.tile([P, D, HALF], U32, name=f"pair_words{u}", align_bytes=64) for u in range(2)]
-        for u in range(2):
+        pair_words = [
+            ring.tile([P, D, HALF], U32, name=f"pair_words{u}", tag=tag, align_bytes=64)
+            for u, tag in enumerate(("pair_words", "w1_raw"))
+        ]
+
+        def gather_pairs(u):
             nc.vector.tensor_copy(
                 pair_words[u][:].rearrange("p d v -> p v d"), table_words[:].indirect(offs_sb[:, u * 32 : (u + 1) * 32])
             )
+
+        gather_pairs(0)
+        w1_q = quantize(dealt["w1"][:], H, keep, "w1", 1)
+        gather_pairs(1)
         for t, u in ((0, 0), (1, 0), (0, 1), (1, 1), (2, 0), (2, 1), (3, 0), (3, 1)):
             cols = slice(u * HALF, (u + 1) * HALF)
             for d in range(D):
                 product(h_banks[t][:, cols], w1_q, t, pair_words[u][:, d, :], pair_scales[:, d, cols], d == 0, d == D - 1)
-        deal_half(nc.scalar.copy, w2_raw[1], dealt["w2"], 1)
-        close_words = keep.tile([P, V], U32, name="close_words", align_bytes=64)
+        deal_half(nc.scalar.copy, w2_raw[0], dealt["w2"], 0)
+        close_words = ring.tile([P, V], U32, name="close_words", tag="w1_dealt", align_bytes=64)
         nc.vector.tensor_copy(close_words[:], table_words[:].indirect(close_sb[:]))
+        deal_half(nc.vector.tensor_copy, w2_raw[1], dealt["w2"], 1)
         h = []
         for t in range(PACK):
             h.append(keep.tile([P, V], F32, name=f"h{t}"))
             nc.scalar.copy(h[t][:], h_banks[t][:])
-        w2_q = quantize(dealt["w2"][:], N, keep, "w2", 1)
 
         gathered, rounded, moments, banks, t_q, results, stored = {}, {}, {}, {}, {}, {}, {}
 
@@ -157,8 +157,8 @@ def tile_picked_yfmm_none_po_kernel(tc, x_words, x_scales, w1, t1, t2, t3, w2, o
             for t in range(PACK):
                 product(banks[c][t][:], t_q[l], t, codes[:, cols], scales[:, cols], False, l == 2)
 
-        def deal_t(l, u):
-            deal_half(nc.scalar.copy, t_raw[l][u], dealt[f"t{l + 1}"], u)
+        def deal_t(l, u, copy=nc.scalar.copy):
+            deal_half(copy, t_raw[l][u], dealt[f"t{l + 1}"], u)
 
         def quantize_t(l):
             t_q[l] = quantize(dealt[f"t{l + 1}"][:], N, keep, f"t{l + 1}", 1)
@@ -194,12 +194,13 @@ def tile_picked_yfmm_none_po_kernel(tc, x_words, x_scales, w1, t1, t2, t3, w2, o
         for t in range(PACK):
             for s in range(3):
                 gather(s, t)
+        w2_q = quantize(dealt["w2"][:], N, keep, "w2", 1)
         open_chunk(0)
         for l in range(2):
             deal_t(l, 0)
             deal_t(l, 1)
         round_moments(0, 2, "t2_raw", sc)
-        deal_t(2, 0)
+        deal_t(2, 0, ve)
         deal_t(2, 1)
         quantize_t(0)
         quantize_t(1)

@@ -15,17 +15,23 @@ FP8X4 = mybir.dt.float8_e4m3fn_x4
 
 P = 128
 PACK = 4
+QUADRANTS = 4
+PER_COLUMN = 16
 HALF = 256
-STEPS = [(0, 0, 256), (1, 0, 256), (2, 0, 256), (0, 256, 256), (1, 256, 256), (2, 256, 128), (2, 384, 128)]
-SLOT = [0, 1, 2, 0, 2, 0, 2]
+
 CHUNKS = [(0, 256), (256, 128), (384, 128)]
+STEPS = [(0, 0, 256), (1, 0, 256), (2, 0, 256), (0, 256, 256), (1, 256, 256), (2, 256, 128), (2, 384, 128)]
+BUFFER = [0, 1, 2, 0, 2, 0, 2]
 
 
-def tile_picked_yfmm_none_po_kernel(tc, x_words, x_scales, w1, t1, t2, t3, w2, offs, far1, far2, far3, close, out_0, out_1, out_2):
+def tile_picked_yfmm_none_po_kernel(
+    tc, x_words, x_scales, w1, t1, t2, t3, w2, offs, far1, far2, far3, close, out_0, out_1, out_2
+):
     nc = tc.nc
+    scalar_copy, vector_copy = nc.scalar.copy, nc.vector.tensor_copy
     with ExitStack() as ctx:
         keep = ctx.enter_context(tc.tile_pool(name="keep", bufs=1))
-        ring = ctx.enter_context(tc.tile_pool(name="ring", bufs=1))
+        shared = ctx.enter_context(tc.tile_pool(name="shared", bufs=1))
         psum = ctx.enter_context(tc.psum_pool(name="psum", bufs=2))
 
         def load_list(src, name):
@@ -34,29 +40,30 @@ def tile_picked_yfmm_none_po_kernel(tc, x_words, x_scales, w1, t1, t2, t3, w2, o
             return tile
 
         def load_weight(w, name):
-            raw = ring.tile([P, PACK, 2 * HALF], F32, name=f"{name}_raw", tag=f"{name}_raw", align_bytes=64)
+            raw = shared.tile([P, PACK, 2 * HALF], F32, name=f"{name}_raw", tag=f"{name}_raw", align_bytes=64)
             nc.sync.dma_start(raw[:], w.rearrange("(p j) c -> p j c", j=PACK))
             return [raw[:, :, u * HALF : (u + 1) * HALF] for u in range(2)]
 
-        def deal_half(copy, raw_half, dealt, u):
-            m_cols = slice(u * 64, (u + 1) * 64)
-            copy(
-                dealt[:].rearrange("p (t m j) -> p m j t", t=PACK, j=PACK)[:, m_cols],
-                raw_half.rearrange("p j (m t) -> p m j t", t=PACK),
+        def deal_half(name, u):
+            per_tile = HALF // PACK
+            nc.scalar.copy(
+                dealt[name][:].rearrange("p (t m j) -> p m j t", t=PACK, j=PACK)[:, u * per_tile : (u + 1) * per_tile],
+                raw_halves[name][u].rearrange("p j (m t) -> p m j t", t=PACK),
             )
 
-        def quantize(src, width, pool, name, bufs):
-            codes = pool.tile([P, width], U32, name=f"{name}_codes", align_bytes=64, bufs=bufs)
-            scales = pool.tile([P, width], U8, name=f"{name}_scales", align_bytes=64, bufs=bufs)
+        def quantize(src, width, name):
+            codes = keep.tile([P, width], U32, name=f"{name}_codes", align_bytes=64)
+            scales = keep.tile([P, width], U8, name=f"{name}_scales", align_bytes=64)
             nc.vector.quantize_mx(out=codes[:].bitcast(FP8X4), scales=scales[:], in_=src)
             return codes, scales
 
         def product(acc, weight, t, moving_codes, moving_scales, start, stop):
+            codes, scales = weight
             cols = slice(t * P, (t + 1) * P)
             nc.tensor.matmul_mx(
                 out=acc,
-                lhsT=weight[0][:, cols].bitcast(FP8X4),
-                lhsT_scale=weight[1][:, cols],
+                lhsT=codes[:, cols].bitcast(FP8X4),
+                lhsT_scale=scales[:, cols],
                 rhs=moving_codes.bitcast(FP8X4),
                 rhs_scale=moving_scales,
                 start=start,
@@ -67,78 +74,107 @@ def tile_picked_yfmm_none_po_kernel(tc, x_words, x_scales, w1, t1, t2, t3, w2, o
         nc.vector.memset(table_scales[:].bitcast(I32), 0)
         offs_sb = load_list(offs, "offs_sb")
         close_sb = load_list(close, "close_sb")
-        far_sb = [load_list(far1, "far1_sb")]
-        for q in range(4):
-            (nc.scalar if q % 2 else nc.sync).dma_start(
+        for q in range(QUADRANTS):
+            queue = nc.scalar if q % 2 else nc.sync
+            queue.dma_start(
                 table_scales[32 * q : 32 * q + 4, :].bitcast(I32), x_scales[0][4 * q : 4 * q + 4, :].bitcast(I32)
             )
-        w1_raw = load_weight(w1, "w1")
+        raw_halves = {"w1": load_weight(w1, "w1")}
         table_words = keep.tile([P, T], U32, name="table_words")
-        nc.sync.dma_start(table_words[:].bitcast(I32), x_words[0].rearrange("p n t -> p (n t)").bitcast(I32))
-        w2_raw = load_weight(w2, "w2")
-        far_sb.extend([load_list(far2, "far2_sb"), load_list(far3, "far3_sb")])
-        t_raw = [load_weight(t1, "t1")]
-        t_raw.append(load_weight(t2, "t2"))
-        t_raw.append(load_weight(t3, "t3"))
-
-        dealt = {name: ring.tile([P, PACK * H], BF16, name=f"{name}_dealt", tag=f"{name}_dealt", align_bytes=64) for name in ("w1", "w2", "t1", "t2", "t3")}
+        nc.sync.dma_start(table_words[:].bitcast(I32), x_words[0].rearrange("p n j -> p (n j)").bitcast(I32))
+        raw_halves["w2"] = load_weight(w2, "w2")
+        far_sb = [load_list(far1, "far1_sb"), load_list(far2, "far2_sb"), load_list(far3, "far3_sb")]
+        far_weights = ["t1", "t2", "t3"]
+        for name, w in zip(far_weights, (t1, t2, t3)):
+            raw_halves[name] = load_weight(w, name)
+        dealt = {
+            name: shared.tile([P, PACK * H], BF16, name=f"{name}_dealt", tag=f"{name}_dealt", align_bytes=64)
+            for name in raw_halves
+        }
 
         for u in range(2):
-            deal_half(nc.scalar.copy, w1_raw[u], dealt["w1"], u)
+            deal_half("w1", u)
         picked_scales = keep.tile([P, S], U8, name="picked_scales")
         nc.vector.tensor_copy(picked_scales[:], table_scales[:].indirect(offs_sb[:]))
         close_scales = keep.tile([P, V], U8, name="close_scales", align_bytes=64)
         nc.vector.tensor_copy(close_scales[:], table_scales[:].indirect(close_sb[:]))
         pair_scales = keep.tile([P, D, V], U8, name="pair_scales", align_bytes=64)
-        nc.vector.tensor_copy(pair_scales[:].rearrange("p d v -> p v d"), picked_scales[:].rearrange("p (v d) -> p v d", d=D))
+        nc.vector.tensor_copy(pair_scales[:], picked_scales[:].rearrange("p (v d) -> p d v", d=D))
 
-        h_banks = [psum.tile([P, V], F32, name=f"h_bank{t}", tag=f"bank{t}") for t in range(PACK)]
         pair_words = [
-            ring.tile([P, D, HALF], U32, name=f"pair_words{u}", tag=tag, align_bytes=64)
+            shared.tile([P, D, HALF], U32, name=f"pair_words{u}", tag=tag, align_bytes=64)
             for u, tag in enumerate(("pair_words", "w1_raw"))
         ]
 
         def gather_pairs(u):
+            columns = D * HALF // PER_COLUMN
             nc.vector.tensor_copy(
-                pair_words[u][:].rearrange("p d v -> p v d"), table_words[:].indirect(offs_sb[:, u * 32 : (u + 1) * 32])
+                pair_words[u][:].rearrange("p d v -> p v d"),
+                table_words[:].indirect(offs_sb[:, u * columns : (u + 1) * columns]),
             )
 
         gather_pairs(0)
-        w1_q = quantize(dealt["w1"][:], H, keep, "w1", 1)
+        w1_q = quantize(dealt["w1"][:], H, "w1")
         gather_pairs(1)
-        for t, u in ((0, 0), (1, 0), (0, 1), (1, 1), (2, 0), (2, 1), (3, 0), (3, 1)):
-            cols = slice(u * HALF, (u + 1) * HALF)
-            for d in range(D):
-                product(h_banks[t][:, cols], w1_q, t, pair_words[u][:, d, :], pair_scales[:, d, cols], d == 0, d == D - 1)
-        deal_half(nc.scalar.copy, w2_raw[0], dealt["w2"], 0)
-        close_words = ring.tile([P, V], U32, name="close_words", tag="w1_dealt", align_bytes=64)
+        h_banks = [psum.tile([P, V], F32, name=f"h_bank{t}", tag=f"bank{t}") for t in range(PACK)]
+        for first_tile in range(0, PACK, 2):
+            for u in range(2):
+                leaves = slice(u * HALF, (u + 1) * HALF)
+                for t in (first_tile, first_tile + 1):
+                    for d in range(D):
+                        product(
+                            h_banks[t][:, leaves], w1_q, t, pair_words[u][:, d, :], pair_scales[:, d, leaves],
+                            d == 0, d == D - 1,
+                        )
+        for u in range(2):
+            deal_half("w2", u)
+        close_words = shared.tile([P, V], U32, name="close_words", tag="w1_dealt", align_bytes=64)
         nc.vector.tensor_copy(close_words[:], table_words[:].indirect(close_sb[:]))
-        deal_half(nc.vector.tensor_copy, w2_raw[1], dealt["w2"], 1)
         h = []
         for t in range(PACK):
             h.append(keep.tile([P, V], F32, name=f"h{t}"))
             nc.scalar.copy(h[t][:], h_banks[t][:])
 
-        gathered, rounded, moments, banks, t_q, results, stored = {}, {}, {}, {}, {}, {}, {}
+        gathered, rounded, moments, far_q = {}, {}, {}, {}
+        banks, result, result_bf = {}, {}, {}
+        out_scales = keep.tile([P, V], U8, name="out_scales", align_bytes=64)
 
         def gather(s, t):
             l, v0, n = STEPS[s]
             if s not in gathered:
-                gathered[s] = ring.tile([P, PACK, n], F32, name=f"gathered{s}", tag=f"gathered{SLOT[s]}", align_bytes=64)
-            nc.vector.tensor_copy(gathered[s][:, t, :], h[t][:].indirect(far_sb[l][:, v0 // 16 : (v0 + n) // 16]))
+                gathered[s] = shared.tile(
+                    [P, PACK, n], F32, name=f"gathered{s}", tag=f"gathered{BUFFER[s]}", align_bytes=64
+                )
+            offsets = far_sb[l][:, v0 // PER_COLUMN : (v0 + n) // PER_COLUMN]
+            nc.vector.tensor_copy(gathered[s][:, t, :], h[t][:].indirect(offsets))
+
+        def gather_step(s):
+            for t in range(PACK):
+                gather(s, t)
 
         def weave(copy, src, dst):
+            run = 4 if copy is scalar_copy else 2
             copy(
-                dst.rearrange("p (c i t) -> p c t i", i=4, t=PACK),
-                src[:].rearrange("p t (c i) -> p c t i", i=4),
+                dst.rearrange("p (c i t) -> p c t i", i=run, t=PACK),
+                src[:].rearrange("p t (c i) -> p c t i", i=run),
             )
 
         def round_moments(first, count, tag, copy):
             n = STEPS[first][2]
-            tile = ring.tile([P, count, PACK * n], BF16, name=f"rounded{first}", tag=tag, align_bytes=64)
+            tile = shared.tile([P, count, PACK * n], BF16, name=f"rounded{first}", tag=tag, align_bytes=64)
             for i in range(count):
                 rounded[first + i] = tile[:, i, :]
                 weave(copy, gathered[first + i], rounded[first + i])
+
+        def quantize_moments(s):
+            moments[s] = quantize(rounded[s], STEPS[s][2], f"m{s}")
+
+        def deal_far_weight(l):
+            for u in range(2):
+                deal_half(far_weights[l], u)
+
+        def quantize_far_weight(l):
+            far_q[l] = quantize(dealt[far_weights[l]][:], N, far_weights[l])
 
         def open_chunk(c):
             v0, n = CHUNKS[c]
@@ -146,101 +182,84 @@ def tile_picked_yfmm_none_po_kernel(tc, x_words, x_scales, w1, t1, t2, t3, w2, o
             for t in range(PACK):
                 product(banks[c][t][:], w2_q, t, close_words[:, v0 : v0 + n], close_scales[:, v0 : v0 + n], True, False)
 
-        def quantize_moments(s):
-            moments[s] = quantize(rounded[s], STEPS[s][2], keep, f"m{s}", 1)
-
         def multiply(s, c):
-            l, s0, width = STEPS[s]
+            l, step_v0, step_n = STEPS[s]
             v0, n = CHUNKS[c]
-            cols = slice(v0 - s0, v0 - s0 + n)
+            assert step_v0 <= v0 and v0 + n <= step_v0 + step_n
+            cols = slice(v0 - step_v0, v0 - step_v0 + n)
             codes, scales = moments[s]
             for t in range(PACK):
-                product(banks[c][t][:], t_q[l], t, codes[:, cols], scales[:, cols], False, l == 2)
-
-        def deal_t(l, u, copy=nc.scalar.copy):
-            deal_half(copy, t_raw[l][u], dealt[f"t{l + 1}"], u)
-
-        def quantize_t(l):
-            t_q[l] = quantize(dealt[f"t{l + 1}"][:], N, keep, f"t{l + 1}", 1)
-
-        out_scales = keep.tile([P, V], U8, name="out_scales", align_bytes=64)
+                product(banks[c][t][:], far_q[l], t, codes[:, cols], scales[:, cols], False, l == len(far_weights) - 1)
 
         def drain(c, copies):
             v0, n = CHUNKS[c]
-            result = keep.tile([P, PACK, n], F32, name=f"result{c}")
+            result[c] = keep.tile([P, PACK, n], F32, name=f"result{c}")
             for t in range(PACK):
-                copies[t](result[:, t, :], banks[c][t][:])
-            nc.sync.dma_start(out_0.rearrange("(p t) v -> p t v", t=PACK)[:, :, v0 : v0 + n], result[:])
-            results[c] = keep.tile([P, PACK * n], BF16, name=f"result_bf{c}", align_bytes=64)
-            stored[c] = result
+                copies[t](result[c][:, t, :], banks[c][t][:])
+            nc.sync.dma_start(out_0.rearrange("(p t) v -> p t v", t=PACK)[:, :, v0 : v0 + n], result[c][:])
 
         def round_result(c, copy):
-            weave(copy, stored[c], results[c][:])
+            result_bf[c] = keep.tile([P, PACK * CHUNKS[c][1]], BF16, name=f"result_bf{c}", align_bytes=64)
+            weave(copy, result[c], result_bf[c][:])
 
         def hand_on(c):
             v0, n = CHUNKS[c]
             words = keep.tile([P, n], U32, name=f"out_words{c}", align_bytes=64)
-            nc.vector.quantize_mx(out=words[:].bitcast(FP8X4), scales=out_scales[:, v0 : v0 + n], in_=results[c][:])
+            nc.vector.quantize_mx(out=words[:].bitcast(FP8X4), scales=out_scales[:, v0 : v0 + n], in_=result_bf[c][:])
             nc.sync.dma_start(
-                out_1[0].rearrange("p n t -> p (n t)").bitcast(I32)[:, v0 : v0 + n], words[:].bitcast(I32)
+                out_1[0].rearrange("p n j -> p (n j)").bitcast(I32)[:, v0 : v0 + n], words[:].bitcast(I32)
             )
-
-        sc, ve = nc.scalar.copy, nc.vector.tensor_copy
-
-        def gather_all(s):
-            for t in range(PACK):
-                gather(s, t)
 
         for t in range(PACK):
             for s in range(3):
                 gather(s, t)
-        w2_q = quantize(dealt["w2"][:], N, keep, "w2", 1)
+        w2_q = quantize(dealt["w2"][:], N, "w2")
         open_chunk(0)
-        for l in range(2):
-            deal_t(l, 0)
-            deal_t(l, 1)
-        round_moments(0, 2, "t2_raw", sc)
-        deal_t(2, 0, ve)
-        deal_t(2, 1)
-        quantize_t(0)
-        quantize_t(1)
+        deal_far_weight(0)
+        deal_far_weight(1)
+        round_moments(0, 2, "t2_raw", scalar_copy)
+        deal_far_weight(2)
+        quantize_far_weight(0)
+        quantize_far_weight(1)
         quantize_moments(0)
         multiply(0, 0)
-        gather_all(3)
-        round_moments(2, 2, "t3_raw", sc)
+        gather_step(3)
+        round_moments(2, 2, "t3_raw", scalar_copy)
         quantize_moments(1)
         multiply(1, 0)
-        quantize_t(2)
+        quantize_far_weight(2)
         quantize_moments(2)
         multiply(2, 0)
-        gather_all(4)
+
+        gather_step(4)
         open_chunk(1)
-        drain(0, [sc] * 4)
+        drain(0, [scalar_copy] * PACK)
         open_chunk(2)
         quantize_moments(3)
-        round_moments(4, 1, "t3_raw", sc)
+        round_moments(4, 1, "t3_raw", scalar_copy)
         multiply(3, 1)
         multiply(3, 2)
-        gather_all(5)
-        round_moments(5, 1, "rounded5", sc)
-        round_result(0, sc)
+        gather_step(5)
+        round_moments(5, 1, "rounded5", scalar_copy)
+        round_result(0, scalar_copy)
         quantize_moments(4)
         multiply(4, 1)
         multiply(4, 2)
-        gather_all(6)
+        gather_step(6)
+
         quantize_moments(5)
         multiply(5, 1)
-        round_moments(6, 1, f"gathered{SLOT[5]}", ve)
-        drain(1, [sc] * 4)
+        round_moments(6, 1, f"gathered{BUFFER[5]}", vector_copy)
+        drain(1, [scalar_copy] * PACK)
         quantize_moments(6)
         multiply(6, 2)
         hand_on(0)
-        round_result(1, ve)
-        drain(2, [sc, ve, sc, ve])
+        round_result(1, vector_copy)
+        drain(2, [scalar_copy, vector_copy] * (PACK // 2))
         hand_on(1)
-        round_result(2, ve)
+        round_result(2, vector_copy)
         hand_on(2)
-        for q in range(4):
+        for q in range(QUADRANTS):
             queue = nc.scalar if q % 2 else nc.sync
             queue.dma_start(
                 out_2[0][4 * q : 4 * q + 4, :].bitcast(I32), out_scales[32 * q : 32 * q + 4, :].bitcast(I32)

from contextlib import ExitStack

import concourse.mybir as mybir

K, T, S, D, H, N, V = 512, 2048, 1024, 2, 512, 512, 512
FLOPS = 2 * K * H * S + 3 * 2 * H * N * V + 2 * K * N * V

F32 = mybir.dt.float32
BF16 = mybir.dt.bfloat16
I32 = mybir.dt.int32
U32 = mybir.dt.uint32
U16 = mybir.dt.uint16
U8 = mybir.dt.uint8
FP8X4 = mybir.dt.float8_e4m3fn_x4

P = 128
PACK = 4
QUADRANTS = 4
PER_COLUMN = 16
HALF = 256

CHUNKS = [(0, 256), (256, 128), (384, 128)]
STEPS = [(0, 0, 256), (1, 0, 256), (2, 0, 256), (0, 256, 256), (1, 256, 256), (2, 256, 128), (2, 384, 128)]
BUFFER = [0, 1, 2, 0, 2, 0, 2]


def tile_picked_yfmm_none_po_kernel(
    tc, x_words, x_scales, w1, t1, t2, t3, w2, offs, far1, far2, far3, close, out_0, out_1, out_2
):
    nc = tc.nc
    scalar_copy, vector_copy = nc.scalar.copy, nc.vector.tensor_copy
    with ExitStack() as ctx:
        keep = ctx.enter_context(tc.tile_pool(name="keep", bufs=1))
        shared = ctx.enter_context(tc.tile_pool(name="shared", bufs=1))
        psum = ctx.enter_context(tc.psum_pool(name="psum", bufs=2))

        def load_list(src, name):
            tile = keep.tile(list(src.shape), U16, name=name)
            nc.sync.dma_start(tile[:], src)
            return tile

        def load_weight(w, name):
            raw = shared.tile([P, PACK, 2 * HALF], F32, name=f"{name}_raw", tag=f"{name}_raw", align_bytes=64)
            nc.sync.dma_start(raw[:], w.rearrange("(p j) c -> p j c", j=PACK))
            return [raw[:, :, u * HALF : (u + 1) * HALF] for u in range(2)]

        def deal_half(name, u):
            per_tile = HALF // PACK
            nc.scalar.copy(
                dealt[name][:].rearrange("p (t m j) -> p m j t", t=PACK, j=PACK)[:, u * per_tile : (u + 1) * per_tile],
                raw_halves[name][u].rearrange("p j (m t) -> p m j t", t=PACK),
            )

        def quantize(src, width, name):
            codes = keep.tile([P, width], U32, name=f"{name}_codes", align_bytes=64)
            scales = keep.tile([P, width], U8, name=f"{name}_scales", align_bytes=64)
            nc.vector.quantize_mx(out=codes[:].bitcast(FP8X4), scales=scales[:], in_=src)
            return codes, scales

        def product(acc, weight, t, moving_codes, moving_scales, start, stop):
            codes, scales = weight
            cols = slice(t * P, (t + 1) * P)
            nc.tensor.matmul_mx(
                out=acc,
                lhsT=codes[:, cols].bitcast(FP8X4),
                lhsT_scale=scales[:, cols],
                rhs=moving_codes.bitcast(FP8X4),
                rhs_scale=moving_scales,
                start=start,
                stop=stop,
            )

        table_scales = keep.tile([P, T], U8, name="table_scales")
        nc.vector.memset(table_scales[:].bitcast(I32), 0)
        offs_sb = load_list(offs, "offs_sb")
        close_sb = load_list(close, "close_sb")
        for q in range(QUADRANTS):
            queue = nc.scalar if q % 2 else nc.sync
            queue.dma_start(
                table_scales[32 * q : 32 * q + 4, :].bitcast(I32), x_scales[0][4 * q : 4 * q + 4, :].bitcast(I32)
            )
        raw_halves = {"w1": load_weight(w1, "w1")}
        table_words = keep.tile([P, T], U32, name="table_words")
        nc.sync.dma_start(table_words[:].bitcast(I32), x_words[0].rearrange("p n j -> p (n j)").bitcast(I32))
        raw_halves["w2"] = load_weight(w2, "w2")
        far_sb = [load_list(far1, "far1_sb"), load_list(far2, "far2_sb"), load_list(far3, "far3_sb")]
        far_weights = ["t1", "t2", "t3"]
        for name, w in zip(far_weights, (t1, t2, t3)):
            raw_halves[name] = load_weight(w, name)
        dealt = {
            name: shared.tile([P, PACK * H], BF16, name=f"{name}_dealt", tag=f"{name}_dealt", align_bytes=64)
            for name in raw_halves
        }

        for u in range(2):
            deal_half("w1", u)
        picked_scales = keep.tile([P, S], U8, name="picked_scales")
        nc.vector.tensor_copy(picked_scales[:], table_scales[:].indirect(offs_sb[:]))
        close_scales = keep.tile([P, V], U8, name="close_scales", align_bytes=64)
        nc.vector.tensor_copy(close_scales[:], table_scales[:].indirect(close_sb[:]))
        pair_scales = keep.tile([P, D, V], U8, name="pair_scales", align_bytes=64)
        nc.vector.tensor_copy(pair_scales[:], picked_scales[:].rearrange("p (v d) -> p d v", d=D))

        pair_words = [
            shared.tile([P, D, HALF], U32, name=f"pair_words{u}", tag=tag, align_bytes=64)
            for u, tag in enumerate(("pair_words", "w1_raw"))
        ]

        def gather_pairs(u):
            columns = D * HALF // PER_COLUMN
            nc.vector.tensor_copy(
                pair_words[u][:].rearrange("p d v -> p v d"),
                table_words[:].indirect(offs_sb[:, u * columns : (u + 1) * columns]),
            )

        gather_pairs(0)
        w1_q = quantize(dealt["w1"][:], H, "w1")
        gather_pairs(1)
        h_banks = [psum.tile([P, V], F32, name=f"h_bank{t}", tag=f"bank{t}") for t in range(PACK)]
        for first_tile in range(0, PACK, 2):
            for u in range(2):
                leaves = slice(u * HALF, (u + 1) * HALF)
                for t in (first_tile, first_tile + 1):
                    for d in range(D):
                        product(
                            h_banks[t][:, leaves], w1_q, t, pair_words[u][:, d, :], pair_scales[:, d, leaves],
                            d == 0, d == D - 1,
                        )
        for u in range(2):
            deal_half("w2", u)
        close_words = shared.tile([P, V], U32, name="close_words", tag="w1_dealt", align_bytes=64)
        nc.vector.tensor_copy(close_words[:], table_words[:].indirect(close_sb[:]))
        h = []
        for t in range(PACK):
            h.append(keep.tile([P, V], F32, name=f"h{t}"))
            nc.scalar.copy(h[t][:], h_banks[t][:])

        gathered, rounded, moments, far_q = {}, {}, {}, {}
        banks, result, result_bf = {}, {}, {}
        out_scales = keep.tile([P, V], U8, name="out_scales", align_bytes=64)

        def gather(s, t):
            l, v0, n = STEPS[s]
            if s not in gathered:
                gathered[s] = shared.tile(
                    [P, PACK, n], F32, name=f"gathered{s}", tag=f"gathered{BUFFER[s]}", align_bytes=64
                )
            offsets = far_sb[l][:, v0 // PER_COLUMN : (v0 + n) // PER_COLUMN]
            nc.vector.tensor_copy(gathered[s][:, t, :], h[t][:].indirect(offsets))

        def gather_step(s):
            for t in range(PACK):
                gather(s, t)

        def weave(copy, src, dst):
            run = 4 if copy is scalar_copy else 2
            copy(
                dst.rearrange("p (c i t) -> p c t i", i=run, t=PACK),
                src[:].rearrange("p t (c i) -> p c t i", i=run),
            )

        def round_moments(first, count, tag, copy):
            n = STEPS[first][2]
            tile = shared.tile([P, count, PACK * n], BF16, name=f"rounded{first}", tag=tag, align_bytes=64)
            for i in range(count):
                rounded[first + i] = tile[:, i, :]
                weave(copy, gathered[first + i], rounded[first + i])

        def quantize_moments(s):
            moments[s] = quantize(rounded[s], STEPS[s][2], f"m{s}")

        def deal_far_weight(l):
            for u in range(2):
                deal_half(far_weights[l], u)

        def quantize_far_weight(l):
            far_q[l] = quantize(dealt[far_weights[l]][:], N, far_weights[l])

        def open_chunk(c):
            v0, n = CHUNKS[c]
            banks[c] = [psum.tile([P, n], F32, name=f"out_bank{t}", tag=f"bank{t}") for t in range(PACK)]
            for t in range(PACK):
                product(banks[c][t][:], w2_q, t, close_words[:, v0 : v0 + n], close_scales[:, v0 : v0 + n], True, False)

        def multiply(s, c):
            l, step_v0, step_n = STEPS[s]
            v0, n = CHUNKS[c]
            assert step_v0 <= v0 and v0 + n <= step_v0 + step_n
            cols = slice(v0 - step_v0, v0 - step_v0 + n)
            codes, scales = moments[s]
            for t in range(PACK):
                product(banks[c][t][:], far_q[l], t, codes[:, cols], scales[:, cols], False, l == len(far_weights) - 1)

        def drain(c, copies):
            v0, n = CHUNKS[c]
            result[c] = keep.tile([P, PACK, n], F32, name=f"result{c}")
            for t in range(PACK):
                copies[t](result[c][:, t, :], banks[c][t][:])
            nc.sync.dma_start(out_0.rearrange("(p t) v -> p t v", t=PACK)[:, :, v0 : v0 + n], result[c][:])

        def round_result(c, copy):
            result_bf[c] = keep.tile([P, PACK * CHUNKS[c][1]], BF16, name=f"result_bf{c}", align_bytes=64)
            weave(copy, result[c], result_bf[c][:])

        def hand_on(c):
            v0, n = CHUNKS[c]
            words = keep.tile([P, n], U32, name=f"out_words{c}", align_bytes=64)
            nc.vector.quantize_mx(out=words[:].bitcast(FP8X4), scales=out_scales[:, v0 : v0 + n], in_=result_bf[c][:])
            nc.sync.dma_start(
                out_1[0].rearrange("p n j -> p (n j)").bitcast(I32)[:, v0 : v0 + n], words[:].bitcast(I32)
            )

        for t in range(PACK):
            for s in range(3):
                gather(s, t)
        w2_q = quantize(dealt["w2"][:], N, "w2")
        open_chunk(0)
        deal_far_weight(0)
        deal_far_weight(1)
        round_moments(0, 2, "t2_raw", scalar_copy)
        deal_far_weight(2)
        quantize_far_weight(0)
        quantize_far_weight(1)
        quantize_moments(0)
        multiply(0, 0)
        gather_step(3)
        round_moments(2, 2, "t3_raw", scalar_copy)
        quantize_moments(1)
        multiply(1, 0)
        quantize_far_weight(2)
        quantize_moments(2)
        multiply(2, 0)

        gather_step(4)
        open_chunk(1)
        drain(0, [scalar_copy] * PACK)
        open_chunk(2)
        quantize_moments(3)
        round_moments(4, 1, "t3_raw", scalar_copy)
        multiply(3, 1)
        multiply(3, 2)
        gather_step(5)
        round_moments(5, 1, "rounded5", scalar_copy)
        round_result(0, scalar_copy)
        quantize_moments(4)
        multiply(4, 1)
        multiply(4, 2)
        gather_step(6)

        quantize_moments(5)
        multiply(5, 1)
        round_moments(6, 1, f"gathered{BUFFER[5]}", vector_copy)
        drain(1, [scalar_copy] * PACK)
        quantize_moments(6)
        multiply(6, 2)
        hand_on(0)
        round_result(1, vector_copy)
        drain(2, [scalar_copy, vector_copy] * (PACK // 2))
        hand_on(1)
        round_result(2, vector_copy)
        hand_on(2)
        for q in range(QUADRANTS):
            queue = nc.scalar if q % 2 else nc.sync
            queue.dma_start(
                out_2[0][4 * q : 4 * q + 4, :].bitcast(I32), out_scales[32 * q : 32 * q + 4, :].bitcast(I32)
            )
